import numpy as np, ml_dtypes
CORES = [23,119,17,113]
N = 4
K, F = 8, 32
def setup_inputs(rng):
    return {"gr": rng.standard_normal((N, K, 128, N * F), dtype=np.float32).astype(ml_dtypes.bfloat16)}
def setup_inputs_big(rng):
    d = setup_inputs(rng)
    for k in ("gr",): d[k] = (d[k].astype(np.float32) * 1048576.0).astype(d[k].dtype)
    return d
def setup_inputs_small(rng):
    d = setup_inputs(rng)
    for k in ("gr",): d[k] = (d[k].astype(np.float32) * (1 / 1048576.0)).astype(d[k].dtype)
    return d
def reference(gr):
    s = gr.astype(np.float64).sum(axis=(0, 1))
    return {"y": np.stack([s[:, F * r:F * r + F] for r in range(N)]).astype(np.float32 if gr.dtype != np.float64 else np.float64)}

@@ -1,0 +1,114 @@
+from concourse.bass import DstId, RemoteDMATransfer
+from concourse.mybir import AluOpType
+
+N, K, F, P = 4, 8, 32, 128
+RP = K
+G = P // RP
+WW = P + RP
+NEAR_ENGINES = 4
+
+SCRATCH = {
+    "x": ("sbuf", [P, RP, N, F], "bfloat16"),
+    "pat": ("sbuf", [P, G * G], "bfloat16"),
+    "eye": ("sbuf", [P, G], "bfloat16"),
+    "sel": ("sbuf", [P, WW], "bfloat16"),
+    "pnear": ("psum", [P, 512], "float32"),
+    "pfar": ("psum", [P, 512], "float32"),
+    "snear": ("sbuf", [P, F], "float32"),
+    "sfar": ("sbuf", [P, N * F], "float32"),
+    "land": ("sbuf", [P, N * F], "float32"),
+    "acc": ("sbuf", [P, N * F], "float32"),
+}
+SEMAPHORES = ["ld", "ms", "vd", "wz", "mma", "mmb", "rda", "rdb", "sent", "ad", "st"] + ["arr%d" % i for i in range(N)]
+
+
+def _engines(mask):
+    return [e for e in range(mask.bit_length()) if (mask >> e) & 1]
+
+
+def _mask(engines):
+    return sum(1 << e for e in engines)
+
+
+def _blocks(bl):
+    if len(bl) == 1:
+        return slice(bl[0], bl[0] + 1)
+    step = bl[1] - bl[0]
+    assert all(b - a == step for a, b in zip(bl, bl[1:]))
+    return slice(bl[0], bl[-1] + 1, step)
+
+
+def rank_program(g, core, T, topo):
+    rank = T.rank_of(core)
+    if rank is None:
+        return
+    S = T.sem
+    cores = list(T.cores)
+    others = [r for r in range(N) if r != rank]
+    assert all(topo.may_write(core, cores[r]) for r in others)
+    near = [r for r in others if topo.chip(cores[r]) == topo.chip(core)]
+    far = [r for r in others if topo.chip(cores[r]) != topo.chip(core)]
+    home = sorted(near + [rank])
+
+    pool = _engines(topo.mask(core, cores[far[0]]))
+    share = len(pool) // len(far)
+    far_mask = {r: _mask(pool[i * share:(i + 1) * share]) for i, r in enumerate(far)}
+    free = [e for e in _engines(topo.mask(core, cores[near[0]])) if e not in pool]
+    near_eng = free[::len(free) // NEAR_ENGINES][:NEAR_ENGINES]
+
+    g.sync.dma_start(T.x[:], T.gr[:]).then_inc(S.ld, 16)
+
+    v = g.vector
+    v.memset(T.pat[0:P // G, :], 0.0).then_inc(S.ms, 1)
+    v.memset(T.sel[:, :], 0.0).then_inc(S.wz, 1)
+    v.wait_ge(S.ms, 1)
+    v.memset(T.pat[0:P // G, 0:G * G:G + 1], 1.0).then_inc(S.ms, 1)
+    g.scalar.wait_ge(S.ms, 2)
+    g.scalar.dma_start(T.eye[:, :], T.pat[0:P // G, :]).then_inc(S.vd, 16)
+    v.wait_ge(S.vd, 16)
+    v.wait_ge(S.wz, 1)
+    v.tensor_copy(T.sel[:, RP - 1:RP - 1 + P:RP], T.eye[:, :]).then_inc(S.wz, 1)
+
+    pe = g.tensor
+    pe.wait_ge(S.ld, 16)
+    pe.wait_ge(S.wz, 2)
+    for bl, ps, sem in ((home, T.pnear, S.mma), (far, T.pfar, S.mmb)):
+        for c in range(RP):
+            mm = pe.matmul(ps[:, 0:len(bl) * F], T.sel[:, RP - 1 - c:RP - 1 - c + P], T.x[:, c, _blocks(bl), :],
+                           c == 0, c == RP - 1)
+        mm.then_inc(sem, 1)
+
+    i_near, i_own = home.index(near[0]), home.index(rank)
+    v.wait_ge(S.mma, 1)
+    v.tensor_copy(T.snear[:, :], T.pnear[:, i_near * F:(i_near + 1) * F]).then_inc(S.rda, 1)
+    v.wait_ge(S.mmb, 1)
+    v.tensor_copy(T.sfar[:, 0:len(far) * F], T.pfar[:, 0:len(far) * F]).then_inc(S.rdb, 1)
+
+    mine = T.land[:, rank * F:(rank + 1) * F]
+    arr = S["arr%d" % rank]
+    rid, pid, _ = topo.addr(cores[near[0]])
+    g.wait_ge(S.rda, 1)
+    g.remote_dma(out_ap=mine, in_ap=T.snear[:, :], remote_sem=arr, local_sem=S.sent, pid=pid, routing_id=rid,
+                 dma_engine_mask=_mask(near_eng))
+    g.wait_ge(S.rdb, 1)
+    trs = []
+    for i, r in enumerate(far):
+        rid, pid, _ = topo.addr(cores[r])
+        trs.append(RemoteDMATransfer(dst_ids=[DstId(rid=rid, pnc=pid)], dma_engine_mask=far_mask[r], remote_sem=arr,
+                                     src=T.sfar[:, i * F:(i + 1) * F], dst=mine))
+    g.remote_dma_fused(trs, local_sem=S.sent)
+
+    order = near + sorted(far, key=lambda r: topo.die(cores[r]) != topo.die(core))
+    count = {r: (len(near_eng) if r in near else share) for r in others}
+    prev = T.pnear[:, i_own * F:(i_own + 1) * F]
+    for i, r in enumerate(order):
+        v.wait_ge(S["arr%d" % r], count[r])
+        if i:
+            v.wait_ge(S.ad, i)
+        nxt = T.acc[:, i * F:(i + 1) * F]
+        v.tensor_tensor(nxt, prev, T.land[:, r * F:(r + 1) * F], AluOpType.add).then_inc(S.ad, 1)
+        prev = nxt
+    g.sync.wait_ge(S.ad, len(order))
+    g.sync.dma_start(T.y[:, :], prev).then_inc(S.st, 16)
+    g.sync.wait_ge(S.st, 16)
+    g.wait_ge(S.sent, len(near_eng) + share * len(far))

@@ -9,8 +9,7 @@ NEAR_ENGINES = 4
 
 SCRATCH = {
     "x": ("sbuf", [P, RP, N, F], "bfloat16"),
-    "pat": ("sbuf", [P, G * G], "bfloat16"),
-    "eye": ("sbuf", [P, G], "bfloat16"),
+    "st": ("sbuf", [P, G + 1], "bfloat16"),
     "sel": ("sbuf", [P, WW], "bfloat16"),
     "pnear": ("psum", [P, 512], "float32"),
     "pfar": ("psum", [P, 512], "float32"),
@@ -19,7 +18,7 @@ SCRATCH = {
     "land": ("sbuf", [P, N * F], "float32"),
     "acc": ("sbuf", [P, N * F], "float32"),
 }
-SEMAPHORES = ["ld", "ms", "vd", "wz", "mma", "mmb", "rda", "rdb", "sent", "ad", "st"] + ["arr%d" % i for i in range(N)]
+SEMAPHORES = ["ld", "ms", "wz", "mma", "mmb", "rda", "rdb", "sent", "ad", "st"] + ["arr%d" % i for i in range(N)]
 
 
 def _engines(mask):
@@ -56,21 +55,22 @@ def rank_program(g, core, T, topo):
     free = [e for e in _engines(topo.mask(core, cores[near[0]])) if e not in pool]
     near_eng = free[::len(free) // NEAR_ENGINES][:NEAR_ENGINES]
 
-    g.sync.dma_start(T.x[:], T.gr[:]).then_inc(S.ld, 16)
+    for k in range(K):
+        q = g.sync if k % 2 == 0 else g.scalar
+        q.dma_start(T.x[k:P:K], T.gr[k]).then_inc(S.ld, 16)
 
     v = g.vector
-    v.memset(T.pat[0:P // G, :], 0.0).then_inc(S.ms, 1)
+    v.memset(T.st[:, :], 0.0).then_inc(S.ms, 1)
     v.memset(T.sel[:, :], 0.0).then_inc(S.wz, 1)
     v.wait_ge(S.ms, 1)
-    v.memset(T.pat[0:P // G, 0:G * G:G + 1], 1.0).then_inc(S.ms, 1)
-    g.scalar.wait_ge(S.ms, 2)
-    g.scalar.dma_start(T.eye[:, :], T.pat[0:P // G, :]).then_inc(S.vd, 16)
-    v.wait_ge(S.vd, 16)
+    for j in range(G):
+        v.memset(T.st[0:K * (j + 1), j + 1:j + 2], 1.0).then_inc(S.ms, 1)
+    v.wait_ge(S.ms, G + 1)
     v.wait_ge(S.wz, 1)
-    v.tensor_copy(T.sel[:, RP - 1:RP - 1 + P:RP], T.eye[:, :]).then_inc(S.wz, 1)
+    v.tensor_tensor(T.sel[:, RP - 1:RP - 1 + P:RP], T.st[:, 1:G + 1], T.st[:, 0:G], AluOpType.subtract).then_inc(S.wz, 1)
 
     pe = g.tensor
-    pe.wait_ge(S.ld, 16)
+    pe.wait_ge(S.ld, 16 * K)
     pe.wait_ge(S.wz, 2)
     for bl, ps, sem in ((home, T.pnear, S.mma), (far, T.pfar, S.mmb)):
         for c in range(RP):

@@ -5,20 +5,26 @@ N, K, F, P = 4, 8, 32, 128
 RP = K
 G = P // RP
 WW = P + RP
-NEAR_ENGINES = 4
 
 SCRATCH = {
+    "raw": ("sbuf", [P, F], "bfloat16"),
     "x": ("sbuf", [P, RP, N, F], "bfloat16"),
-    "st": ("sbuf", [P, G + 1], "bfloat16"),
+    "ramp": ("sbuf", [P, G + 1], "bfloat16"),
+    "stlt": ("sbuf", [P, G + 1], "bfloat16"),
+    "stle": ("sbuf", [P, G + 1], "bfloat16"),
     "sel": ("sbuf", [P, WW], "bfloat16"),
-    "pnear": ("psum", [P, 512], "float32"),
+    "sell": ("sbuf", [P, WW], "bfloat16"),
     "pfar": ("psum", [P, 512], "float32"),
-    "snear": ("sbuf", [P, F], "float32"),
+    "pnear": ("psum", [P, 512], "float32"),
+    "pown": ("psum", [P, 512], "float32"),
     "sfar": ("sbuf", [P, N * F], "float32"),
+    "snear": ("sbuf", [P, F], "float32"),
+    "landr": ("sbuf", [P, F], "bfloat16"),
+    "rawf": ("sbuf", [P, F], "float32"),
     "land": ("sbuf", [P, N * F], "float32"),
     "acc": ("sbuf", [P, N * F], "float32"),
 }
-SEMAPHORES = ["ld", "ms", "wz", "mma", "mmb", "rda", "rdb", "sent", "ad", "st"] + ["arr%d" % i for i in range(N)]
+SEMAPHORES = ["ldr", "ld", "ms", "wz", "mf", "mn", "mo", "rf", "rn", "cv", "sent", "ad", "st", "arre"] + ["arr%d" % i for i in range(N)]
 
 
 def _engines(mask):
@@ -47,68 +53,76 @@ def rank_program(g, core, T, topo):
     assert all(topo.may_write(core, cores[r]) for r in others)
     near = [r for r in others if topo.chip(cores[r]) == topo.chip(core)]
     far = [r for r in others if topo.chip(cores[r]) != topo.chip(core)]
-    home = sorted(near + [rank])
+    nb = near[0]
 
     pool = _engines(topo.mask(core, cores[far[0]]))
+    assert all((topo.mask(core, cores[nb]) >> e) & 1 for e in pool)
     share = len(pool) // len(far)
     far_mask = {r: _mask(pool[i * share:(i + 1) * share]) for i, r in enumerate(far)}
-    free = [e for e in _engines(topo.mask(core, cores[near[0]])) if e not in pool]
-    near_eng = free[::len(free) // NEAR_ENGINES][:NEAR_ENGINES]
 
+    g.sync.dma_start(T.raw[:, :], T.gr[0, :, nb * F:(nb + 1) * F]).then_inc(S.ldr, 16)
     for k in range(K):
         q = g.sync if k % 2 == 0 else g.scalar
         q.dma_start(T.x[k:P:K], T.gr[k]).then_inc(S.ld, 16)
 
     v = g.vector
-    v.memset(T.st[:, :], 0.0).then_inc(S.ms, 1)
+    g.iota(T.ramp[:, :], [[K, G + 1]], 0, -1, allow_small_or_imprecise_dtypes=True).then_inc(S.ms, 1)
     v.memset(T.sel[:, :], 0.0).then_inc(S.wz, 1)
+    v.memset(T.sell[:, :], 0.0).then_inc(S.wz, 1)
     v.wait_ge(S.ms, 1)
-    for j in range(G):
-        v.memset(T.st[0:K * (j + 1), j + 1:j + 2], 1.0).then_inc(S.ms, 1)
-    v.wait_ge(S.ms, G + 1)
-    v.wait_ge(S.wz, 1)
-    v.tensor_tensor(T.sel[:, RP - 1:RP - 1 + P:RP], T.st[:, 1:G + 1], T.st[:, 0:G], AluOpType.subtract).then_inc(S.wz, 1)
+    v.tensor_scalar(T.stlt[:, :], T.ramp[:, :], 0.0, None, AluOpType.is_gt).then_inc(S.ms, 1)
+    v.tensor_scalar(T.stle[:, :], T.ramp[:, :], 0.0, None, AluOpType.is_ge).then_inc(S.ms, 1)
+    v.wait_ge(S.ms, 3)
+    v.wait_ge(S.wz, 2)
+    v.tensor_tensor(T.sel[:, RP - 1:RP - 1 + P:RP], T.stlt[:, 1:G + 1], T.stlt[:, 0:G], AluOpType.subtract).then_inc(S.wz, 1)
+    v.tensor_tensor(T.sell[:, RP - 1:RP - 1 + P:RP], T.stlt[:, 1:G + 1], T.stle[:, 0:G], AluOpType.subtract).then_inc(S.wz, 1)
+
+    rid_n, pid_n, _ = topo.addr(cores[nb])
+    g.wait_ge(S.ldr, 16)
+    g.remote_dma(out_ap=T.landr[:, :], in_ap=T.raw[:, :], remote_sem=S.arre, local_sem=S.sent, pid=pid_n, routing_id=rid_n,
+                 dma_engine_mask=_mask(pool))
 
     pe = g.tensor
     pe.wait_ge(S.ld, 16 * K)
-    pe.wait_ge(S.wz, 2)
-    for bl, ps, sem in ((home, T.pnear, S.mma), (far, T.pfar, S.mmb)):
+    pe.wait_ge(S.wz, 4)
+    for bl, w, ps, sem in ((far, T.sel, T.pfar, S.mf), (near, T.sell, T.pnear, S.mn), ([rank], T.sel, T.pown, S.mo)):
         for c in range(RP):
-            mm = pe.matmul(ps[:, 0:len(bl) * F], T.sel[:, RP - 1 - c:RP - 1 - c + P], T.x[:, c, _blocks(bl), :],
-                           c == 0, c == RP - 1)
+            mm = pe.matmul(ps[:, 0:len(bl) * F], w[:, RP - 1 - c:RP - 1 - c + P], T.x[:, c, _blocks(bl), :], c == 0, c == RP - 1)
         mm.then_inc(sem, 1)
 
-    i_near, i_own = home.index(near[0]), home.index(rank)
-    v.wait_ge(S.mma, 1)
-    v.tensor_copy(T.snear[:, :], T.pnear[:, i_near * F:(i_near + 1) * F]).then_inc(S.rda, 1)
-    v.wait_ge(S.mmb, 1)
-    v.tensor_copy(T.sfar[:, 0:len(far) * F], T.pfar[:, 0:len(far) * F]).then_inc(S.rdb, 1)
+    v.wait_ge(S.mf, 1)
+    v.tensor_copy(T.sfar[:, 0:len(far) * F], T.pfar[:, 0:len(far) * F]).then_inc(S.rf, 1)
+    v.wait_ge(S.mn, 1)
+    v.tensor_copy(T.snear[:, :], T.pnear[:, 0:F]).then_inc(S.rn, 1)
 
     mine = T.land[:, rank * F:(rank + 1) * F]
     arr = S["arr%d" % rank]
-    rid, pid, _ = topo.addr(cores[near[0]])
-    g.wait_ge(S.rda, 1)
-    g.remote_dma(out_ap=mine, in_ap=T.snear[:, :], remote_sem=arr, local_sem=S.sent, pid=pid, routing_id=rid,
-                 dma_engine_mask=_mask(near_eng))
-    g.wait_ge(S.rdb, 1)
+    g.wait_ge(S.rf, 1)
     trs = []
     for i, r in enumerate(far):
         rid, pid, _ = topo.addr(cores[r])
         trs.append(RemoteDMATransfer(dst_ids=[DstId(rid=rid, pnc=pid)], dma_engine_mask=far_mask[r], remote_sem=arr,
                                      src=T.sfar[:, i * F:(i + 1) * F], dst=mine))
     g.remote_dma_fused(trs, local_sem=S.sent)
+    g.wait_ge(S.rn, 1)
+    g.remote_dma(out_ap=mine, in_ap=T.snear[:, :], remote_sem=arr, local_sem=S.sent, pid=pid_n, routing_id=rid_n,
+                 dma_engine_mask=_mask(pool))
 
-    order = near + sorted(far, key=lambda r: topo.die(cores[r]) != topo.die(core))
-    count = {r: (len(near_eng) if r in near else share) for r in others}
-    prev = T.pnear[:, i_own * F:(i_own + 1) * F]
+    v.wait_ge(S.arre, len(pool))
+    v.tensor_copy(T.rawf[:, :], T.landr[:, :]).then_inc(S.cv, 1)
+    v.wait_ge(S.mo, 1)
+    v.wait_ge(S.cv, 1)
+    v.tensor_tensor(T.acc[:, 0:F], T.pown[:, 0:F], T.rawf[:, :], AluOpType.add).then_inc(S.ad, 1)
+    order = sorted(far, key=lambda r: topo.die(cores[r]) != topo.die(core)) + near
+    count = {r: (len(pool) if r in near else share) for r in others}
+    prev = T.acc[:, 0:F]
     for i, r in enumerate(order):
         v.wait_ge(S["arr%d" % r], count[r])
-        if i:
-            v.wait_ge(S.ad, i)
-        nxt = T.acc[:, i * F:(i + 1) * F]
+        v.wait_ge(S.ad, i + 1)
+        nxt = T.acc[:, (i + 1) * F:(i + 2) * F]
         v.tensor_tensor(nxt, prev, T.land[:, r * F:(r + 1) * F], AluOpType.add).then_inc(S.ad, 1)
         prev = nxt
-    g.sync.wait_ge(S.ad, len(order))
+    g.sync.wait_ge(S.ad, len(order) + 1)
     g.sync.dma_start(T.y[:, :], prev).then_inc(S.st, 16)
     g.sync.wait_ge(S.st, 16)
-    g.wait_ge(S.sent, len(near_eng) + share * len(far))
+    g.wait_ge(S.sent, 2 * len(pool) + share * len(far))

from concourse.bass import DstId, RemoteDMATransfer
from concourse.mybir import AluOpType

N, K, F, P = 4, 8, 32, 128
RP = K
G = P // RP
WW = P + RP

SCRATCH = {
    "raw": ("sbuf", [P, F], "bfloat16"),
    "x": ("sbuf", [P, RP, N, F], "bfloat16"),
    "ramp": ("sbuf", [P, G + 1], "bfloat16"),
    "stlt": ("sbuf", [P, G + 1], "bfloat16"),
    "stle": ("sbuf", [P, G + 1], "bfloat16"),
    "sel": ("sbuf", [P, WW], "bfloat16"),
    "sell": ("sbuf", [P, WW], "bfloat16"),
    "pfar": ("psum", [P, 512], "float32"),
    "pnear": ("psum", [P, 512], "float32"),
    "pown": ("psum", [P, 512], "float32"),
    "sfar": ("sbuf", [P, N * F], "float32"),
    "snear": ("sbuf", [P, F], "float32"),
    "landr": ("sbuf", [P, F], "bfloat16"),
    "rawf": ("sbuf", [P, F], "float32"),
    "land": ("sbuf", [P, N * F], "float32"),
    "acc": ("sbuf", [P, N * F], "float32"),
}
SEMAPHORES = ["ldr", "ld", "ms", "wz", "mf", "mn", "mo", "rf", "rn", "cv", "sent", "ad", "st", "arre"] + ["arr%d" % i for i in range(N)]


def _engines(mask):
    return [e for e in range(mask.bit_length()) if (mask >> e) & 1]


def _mask(engines):
    return sum(1 << e for e in engines)


def _blocks(bl):
    if len(bl) == 1:
        return slice(bl[0], bl[0] + 1)
    step = bl[1] - bl[0]
    assert all(b - a == step for a, b in zip(bl, bl[1:]))
    return slice(bl[0], bl[-1] + 1, step)


def rank_program(g, core, T, topo):
    rank = T.rank_of(core)
    if rank is None:
        return
    S = T.sem
    cores = list(T.cores)
    others = [r for r in range(N) if r != rank]
    assert all(topo.may_write(core, cores[r]) for r in others)
    near = [r for r in others if topo.chip(cores[r]) == topo.chip(core)]
    far = [r for r in others if topo.chip(cores[r]) != topo.chip(core)]
    nb = near[0]

    pool = _engines(topo.mask(core, cores[far[0]]))
    assert all((topo.mask(core, cores[nb]) >> e) & 1 for e in pool)
    share = len(pool) // len(far)
    far_mask = {r: _mask(pool[i * share:(i + 1) * share]) for i, r in enumerate(far)}

    g.sync.dma_start(T.raw[:, :], T.gr[0, :, nb * F:(nb + 1) * F]).then_inc(S.ldr, 16)
    for k in range(K):
        q = g.sync if k % 2 == 0 else g.scalar
        q.dma_start(T.x[k:P:K], T.gr[k]).then_inc(S.ld, 16)

    v = g.vector
    g.iota(T.ramp[:, :], [[K, G + 1]], 0, -1, allow_small_or_imprecise_dtypes=True).then_inc(S.ms, 1)
    v.memset(T.sel[:, :], 0.0).then_inc(S.wz, 1)
    v.memset(T.sell[:, :], 0.0).then_inc(S.wz, 1)
    v.wait_ge(S.ms, 1)
    v.tensor_scalar(T.stlt[:, :], T.ramp[:, :], 0.0, None, AluOpType.is_gt).then_inc(S.ms, 1)
    v.tensor_scalar(T.stle[:, :], T.ramp[:, :], 0.0, None, AluOpType.is_ge).then_inc(S.ms, 1)
    v.wait_ge(S.ms, 3)
    v.wait_ge(S.wz, 2)
    v.tensor_tensor(T.sel[:, RP - 1:RP - 1 + P:RP], T.stlt[:, 1:G + 1], T.stlt[:, 0:G], AluOpType.subtract).then_inc(S.wz, 1)
    v.tensor_tensor(T.sell[:, RP - 1:RP - 1 + P:RP], T.stlt[:, 1:G + 1], T.stle[:, 0:G], AluOpType.subtract).then_inc(S.wz, 1)

    rid_n, pid_n, _ = topo.addr(cores[nb])
    g.wait_ge(S.ldr, 16)
    g.remote_dma(out_ap=T.landr[:, :], in_ap=T.raw[:, :], remote_sem=S.arre, local_sem=S.sent, pid=pid_n, routing_id=rid_n,
                 dma_engine_mask=_mask(pool))

    pe = g.tensor
    pe.wait_ge(S.ld, 16 * K)
    pe.wait_ge(S.wz, 4)
    for bl, w, ps, sem in ((far, T.sel, T.pfar, S.mf), (near, T.sell, T.pnear, S.mn), ([rank], T.sel, T.pown, S.mo)):
        for c in range(RP):
            mm = pe.matmul(ps[:, 0:len(bl) * F], w[:, RP - 1 - c:RP - 1 - c + P], T.x[:, c, _blocks(bl), :], c == 0, c == RP - 1)
        mm.then_inc(sem, 1)

    v.wait_ge(S.mf, 1)
    v.tensor_copy(T.sfar[:, 0:len(far) * F], T.pfar[:, 0:len(far) * F]).then_inc(S.rf, 1)
    v.wait_ge(S.mn, 1)
    v.tensor_copy(T.snear[:, :], T.pnear[:, 0:F]).then_inc(S.rn, 1)

    mine = T.land[:, rank * F:(rank + 1) * F]
    arr = S["arr%d" % rank]
    g.wait_ge(S.rf, 1)
    trs = []
    for i, r in enumerate(far):
        rid, pid, _ = topo.addr(cores[r])
        trs.append(RemoteDMATransfer(dst_ids=[DstId(rid=rid, pnc=pid)], dma_engine_mask=far_mask[r], remote_sem=arr,
                                     src=T.sfar[:, i * F:(i + 1) * F], dst=mine))
    g.remote_dma_fused(trs, local_sem=S.sent)
    g.wait_ge(S.rn, 1)
    g.remote_dma(out_ap=mine, in_ap=T.snear[:, :], remote_sem=arr, local_sem=S.sent, pid=pid_n, routing_id=rid_n,
                 dma_engine_mask=_mask(pool))

    v.wait_ge(S.arre, len(pool))
    v.tensor_copy(T.rawf[:, :], T.landr[:, :]).then_inc(S.cv, 1)
    v.wait_ge(S.mo, 1)
    v.wait_ge(S.cv, 1)
    v.tensor_tensor(T.acc[:, 0:F], T.pown[:, 0:F], T.rawf[:, :], AluOpType.add).then_inc(S.ad, 1)
    order = sorted(far, key=lambda r: topo.die(cores[r]) != topo.die(core)) + near
    count = {r: (len(pool) if r in near else share) for r in others}
    prev = T.acc[:, 0:F]
    for i, r in enumerate(order):
        v.wait_ge(S["arr%d" % r], count[r])
        v.wait_ge(S.ad, i + 1)
        nxt = T.acc[:, (i + 1) * F:(i + 2) * F]
        v.tensor_tensor(nxt, prev, T.land[:, r * F:(r + 1) * F], AluOpType.add).then_inc(S.ad, 1)
        prev = nxt
    g.sync.wait_ge(S.ad, len(order) + 1)
    g.sync.dma_start(T.y[:, :], prev).then_inc(S.st, 16)
    g.sync.wait_ge(S.st, 16)
    g.wait_ge(S.sent, 2 * len(pool) + share * len(far))
